import numpy as np, ml_dtypes
CORES = [2,3,42,43,82,83,122,123]
N = 8
BF = ml_dtypes.bfloat16
def f(rng, *shape):
    return (rng.standard_normal(shape, dtype=np.float32) * np.exp2(rng.integers(-2, 3, shape[:-1] + (1,)))).astype(BF)
def wide(rng, *shape):
    v = f(rng, *shape).astype(np.float32); k = shape[:-2] + (1, shape[-1])
    return (v * np.exp2(rng.integers(-6, 7, k)) * (rng.random(k) > 0.0625)).astype(BF)
def gentries(a):
    return np.ascontiguousarray(a.reshape(8, 16, -1).transpose(0, 2, 1)).reshape(8, -1)
def gtable(e):
    e = np.asarray(e); return np.ascontiguousarray(e.reshape(8, -1, 16).transpose(0, 2, 1)).reshape(128, -1).astype(np.int32)
B, M, W, S = 128, 32, 64, 1536
WL, WM, CB, CW = 2, 9, 12, 128
D, FR = 512, 16
MB = M // 16
U, UB = CW // MB, S // MB
def book(rng, v):
    return (v.astype(np.float32) * (1 + rng.random(v.shape, dtype=np.float32))).astype(BF)
def parts(rng, k, s, exact):
    v = rng.integers(WL, WM + 1, k); t = s if exact else min(s, int(np.sum(v)))
    while np.sum(v) != t:
        e = 1 if np.sum(v) < t else -1
        i = np.flatnonzero(v < WM) if e > 0 else np.flatnonzero(v > WL)
        v[rng.permutation(i)[:abs(t - int(np.sum(v)))]] += e
    return v
def widths(rng):
    w = np.zeros((N, 8, B), np.int64)
    for q in range(N):
        for g in range(8):
            w[q, g] = parts(rng, B, UB, False); w[q, g, rng.integers(B)] = WL
    return w
def pick(rng, w, c, cand):
    left = U; lo = int(np.min(w[cand])); out = []
    for i in range(c):
        ok = cand[w[cand] <= left - (c - 1 - i) * lo]
        b = int(ok[rng.integers(len(ok))]); out.append(b); left -= int(w[b])
    return out
def wants(rng, w, uneven=False, full=None):
    L = np.zeros((N, 8, W), np.int64)
    for r in range(N):
        for g in range(8):
            q0 = -1
            own = np.repeat(rng.permutation(N), CB)
            if not uneven: own = rng.permutation(own)
            if full is not None:
                q0 = (r + 1 + g % (N - 1)) % N
                own = np.concatenate([np.full(CB, q0), own[own != q0]])
            c = np.bincount(own[:W], minlength=N); e = []
            for q in range(N):
                if q == q0:
                    e += [q * B + int(b) for b in full[q, g]]
                elif c[q]:
                    cand = np.arange(B)
                    if uneven and rng.random() < 0.5: cand = np.array([int(np.argmin(w[q, g])), int(rng.integers(B))])
                    e += [q * B + b for b in pick(rng, w[q, g], int(c[q]), cand)]
            L[r, g] = rng.permutation(np.array(e))
    return L
def make(rng, w, L, s):
    return {"strm": s.astype(np.int32), "wd": np.stack([gtable(u) for u in w]), "want": np.stack([gtable(u) for u in L]), "dic": book(rng, f(rng, N, 8 * FR, D))}
def setup_inputs(rng):
    w = widths(rng)
    return make(rng, w, wants(rng, w), rng.integers(0, 65536, (N, 8, S)))
def setup_inputs_full(rng):
    w = np.zeros((N, 8, B), np.int64); full = np.zeros((N, 8, CB), np.int64)
    for q in range(N):
        for g in range(8):
            p = np.concatenate([np.array([0, B - 1]), rng.permutation(np.arange(1, B - 1))])
            w[q, g, p[:CB]] = parts(rng, CB, U, True); w[q, g, p[CB:]] = parts(rng, B - CB, UB - U, True); full[q, g] = p[:CB]
    return make(rng, w, wants(rng, w, full=full), rng.integers(0, 65536, (N, 8, S)))
def setup_inputs_uneven(rng):
    w = widths(rng)
    return make(rng, w, wants(rng, w, uneven=True), rng.integers(0, 65536, (N, 8, S)))
def setup_inputs_ends(rng):
    w = np.full((N, 8, B), WL, np.int64); most = min(B - 1, (UB - B * WL) // (WM - WL))
    for q in range(N):
        for g in range(8):
            w[q, g, rng.permutation(B)[:rng.integers(0, most + 1)]] = WM
    s = rng.choice(np.array([0, 0, 1, 32768, 65535, 65535]), (N, 8, S))
    s = np.where(rng.random((N, 8, S)) < 0.25, rng.integers(0, 65536, (N, 8, S)), s)
    return make(rng, w, wants(rng, w), s)
def setup_inputs_spread(rng):
    d = setup_inputs(rng); d["dic"] = book(rng, wide(rng, N, 8 * FR, D)); return d
def check_inputs(d):
    try:
        bad = []
        if d["strm"].min() < 0 or d["strm"].max() > 65535: bad.append("words")
        if not np.isfinite(d["dic"].astype(np.float32)).all(): bad.append("finite")
        w = np.stack([gentries(u) for u in d["wd"]]).astype(np.int64); L = np.stack([gentries(u) for u in d["want"]]).astype(np.int64)
        if w.min() < WL or w.max() > WM: bad.append("widths")
        if (MB * np.sum(w, axis=2) > S).any(): bad.append("words of a column")
        if L.min() < 0 or L.max() >= N * B: return bad + ["wanted blocks"]
        n = np.zeros((N, 8, N), np.int64); m = np.zeros((N, 8, N), np.int64)
        for r in range(N):
            for g in range(8):
                q, b = L[r, g] // B, L[r, g] % B
                np.add.at(n[r, g], q, 1); np.add.at(m[r, g], q, MB * w[q, g, b])
        if n.max() > CB: bad.append("blocks of a pair")
        if m.max() > CW: bad.append("words of a pair")
        return bad
    except Exception:
        return ["shapes"]
def reference(strm, wd, want, dic):
    y = np.zeros((N, 8 * FR, W * M), dic.dtype)
    bit = (strm.astype(np.int64)[..., None] >> np.arange(16) & 1).reshape(N, 8, 16 * S)
    w = np.stack([gentries(wd[q]) for q in range(N)]).astype(np.int64)
    first = M * (np.add.accumulate(w, axis=2) - w)
    for r in range(N):
        L = gentries(want[r]).astype(np.int64)
        for g in range(8):
            q, b = L[g] // B, L[g] % B
            v = w[q, g, b][:, None]; at = first[q, g, b][:, None] + np.arange(M) * v
            code = np.zeros((W, M), np.int64)
            for k in range(WM):
                code += np.where(k < v, bit[q[:, None], g, np.minimum(at + k, 16 * S - 1)], 0) << k
            y[r, FR * g:FR * (g + 1)] = dic[r, FR * g:FR * (g + 1)][:, code.reshape(-1)]
    return {"y": y}

@@ -1,0 +1,315 @@
+from concourse.bass import DstId, RemoteDMATransfer
+from concourse.mybir import AluOpType as OP, ActivationFunctionType as AF
+
+N = 8
+SCRATCH = {
+    "win": ("sbuf", [128, 1536], "int32"),
+    "wantb": ("sbuf", [128, 8], "int32"),
+    "wdb": ("sbuf", [128, 8], "int32"),
+    "dicb": ("sbuf", [128, 512], "bfloat16"),
+    "pi": ("sbuf", [128, 8], "int32"),
+    "pif": ("sbuf", [128, 8], "float32"),
+    "pm": ("sbuf", [128, 8], "int32"),
+    "pf": ("sbuf", [128, 8], "float32"),
+    "g16m": ("sbuf", [128, 8], "float32"),
+    "onec": ("sbuf", [128, 8], "float32"),
+    "maskc": ("sbuf", [128, 8], "float32"),
+    "ccol": ("sbuf", [128, 8], "float32"),
+    "repl": ("sbuf", [128, 16], "uint16"),
+    "xs": ("sbuf", [128, 160], "bfloat16"),
+    "uu": ("sbuf", [128, 128], "bfloat16"),
+    "k8": ("sbuf", [128, 32], "int32"),
+    "cb": ("sbuf", [128, 16], "float32"),
+    "cbs": ("sbuf", [128, 16], "bfloat16"),
+    "seg": ("sbuf", [128, 32], "float32"),
+    "twos": ("sbuf", [128, 16], "float32"),
+    "tbl": ("sbuf", [128, 16], "float32"),
+    "bd": ("sbuf", [128, 128], "bfloat16"),
+    "lf": ("sbuf", [128, 128], "bfloat16"),
+    "ll": ("sbuf", [128, 128], "bfloat16"),
+    "idm": ("sbuf", [128, 128], "bfloat16"),
+    "maskf": ("sbuf", [128, 8], "float32"),
+    "d1e": ("sbuf", [128, 160], "bfloat16"),
+    "d0": ("sbuf", [128, 144], "bfloat16"),
+    "t2": ("sbuf", [128, 144], "bfloat16"),
+    "xl": ("sbuf", [128, 16], "uint16"),
+    "cc": ("sbuf", [128, 256], "bfloat16"),
+    "sm": ("sbuf", [128, 16, 128], "bfloat16"),
+    "qrep": ("sbuf", [128, 32], "int32"),
+    "brep": ("sbuf", [128, 32], "int32"),
+    "epad": ("sbuf", [128, 56], "bfloat16"),
+    "eb": ("sbuf", [128, 32], "bfloat16"),
+    "ss": ("sbuf", [128, 32], "float32"),
+    "lh": ("sbuf", [128, 4, 128], "bfloat16"),
+    "req": ("sbuf", [128, 8], "uint16"),
+    "ownl": ("sbuf", [128, 8], "uint16"),
+    "reqin": ("sbuf", [128, 8], "uint16"),
+    "wb": ("sbuf", [128, 8], "bfloat16"),
+    "wb2": ("sbuf", [128, 8], "bfloat16"),
+    "cs": ("sbuf", [128, 8], "bfloat16"),
+    "lw": ("sbuf", [128, 8], "uint16"),
+    "stl": ("sbuf", [128, 16], "uint16"),
+    "sel": ("sbuf", [128, 16], "uint16"),
+    "loi": ("sbuf", [128, 256], "int32"),
+    "hit": ("sbuf", [128, 256], "float32"),
+    "lob": ("sbuf", [128, 256], "bfloat16"),
+    "hib": ("sbuf", [128, 256], "bfloat16"),
+    "ev": ("sbuf", [128, 2048], "float32"),
+    "ai": ("sbuf", [128, 256], "int32"),
+    "ui": ("sbuf", [128, 256], "int32"),
+    "dd": ("sbuf", [128, 256], "float32"),
+    "outb": ("sbuf", [128, 224], "bfloat16"),
+    "land": ("sbuf", [128, 200], "bfloat16"),
+    "b1": ("sbuf", [128, 32], "int32"),
+    "b2": ("sbuf", [128, 32], "int32"),
+    "b3": ("sbuf", [128, 32], "float32"),
+    "b4": ("sbuf", [128, 32], "float32"),
+    "s2": ("sbuf", [128, 32], "float32"),
+    "pos": ("sbuf", [128, 8], "uint16"),
+    "offs": ("sbuf", [128, 128], "uint16"),
+    "yb": ("sbuf", [128, 2048], "bfloat16"),
+    "ps1": ("psum", [128, 512], "float32"),
+    "ps2": ("psum", [128, 512], "float32"),
+    "ps4": ("psum", [128, 512], "float32"),
+    "ps5": ("psum", [128, 512], "float32"),
+    "e0": ("psum", [128, 512], "float32"),
+    "e1": ("psum", [128, 512], "float32"),
+    "e2": ("psum", [128, 512], "float32"),
+    "e3": ("psum", [128, 512], "float32"),
+}
+SEMAPHORES = ["cv", "ca", "cp", "cg", "lwant", "lwd", "lwin", "ldic", "rq", "dat", "sent", "stored"]
+
+
+def bits(es):
+    m = 0
+    for e in es:
+        m |= 1 << e
+    return m
+
+
+def calls_of(src, cores, topo):
+    near = [c for c in cores if c != src and topo.chip(c) == topo.chip(src)]
+    far = [c for c in cores if topo.chip(c) != topo.chip(src)]
+    far.sort(key=lambda c: topo.same_plane(topo.chip(src), topo.chip(c)))
+    e = topo.engines(src, far[0])
+    first = [(far[0], e[0:4]), (far[1], e[4:6]), (far[2], e[6:8])]
+    second = [(far[4], e[0:2]), (far[5], e[2:4]), (far[3], e[4:8])]
+    free = [x for x in topo.engines(src, near[0]) if x not in e]
+    second.append((near[0], free[0:2]))
+    return [first, second]
+
+
+def rank_program(g, core, T, topo):
+    r = T.rank_of(core)
+    if r is None:
+        return
+    cores = list(T.cores)
+    S = T.sem
+    Q = {"v": g.vector, "a": g.scalar, "p": g.tensor, "g": g, "s": g.sync}
+    cnt = {"v": 0, "a": 0, "p": 0, "g": 0}
+    seen = {}
+
+    def need(q, *toks):
+        best = {}
+        for t in toks:
+            best[t[0]] = max(best.get(t[0], 0), t[1])
+        for name, n in best.items():
+            if seen.get((q, name), 0) < n:
+                Q[q].wait_ge(S[name], n)
+                seen[(q, name)] = n
+
+    def done(q, ins):
+        cnt[q] += 1
+        ins.then_inc(S["c" + q], 1)
+        return ("c" + q, cnt[q])
+
+    V, A, P = g.vector, g.scalar, g.tensor
+
+    def ts(out, in0, s1, op0, s2=None, op1=None, after=()):
+        need("v", *after)
+        if op1 is None:
+            return done("v", V.tensor_scalar(out, in0, s1, None, op0))
+        return done("v", V.tensor_scalar(out, in0, s1, s2, op0, op1))
+
+    def tt(out, in0, in1, op, after=()):
+        need("v", *after)
+        return done("v", V.tensor_tensor(out, in0, in1, op))
+
+    def cp(out, in_, after=()):
+        need("v", *after)
+        return done("v", V.tensor_copy(out, in_))
+
+    def scan(out, d0, d1, init, op0, op1, after=()):
+        need("v", *after)
+        return done("v", V.tensor_tensor_scan(out, d0, d1, init, op0, op1))
+
+    def act(out, in_, func, after=(), **kw):
+        need("a", *after)
+        return done("a", A.activation(out, in_, func, **kw))
+
+    def group(out, pairs, after=()):
+        need("p", *after)
+        for i, (l, rhs) in enumerate(pairs):
+            ins = P.matmul(out, l, rhs, i == 0, i == len(pairs) - 1)
+        return done("p", ins)
+
+    c1 = lambda name: T[name][:, 0:1]
+
+    tail = done("v", V.memset(T.win[:, 1528:1536], 0))
+    g.sync.dma_start(T.wantb[:, 0:4], T.want[:]).then_inc(S.lwant, 16)
+    g.scalar.dma_start(T.wdb[:], T.wd[:]).then_inc(S.lwd, 16)
+    need("s", tail)
+    need("a", tail)
+    for k in range(16):
+        sh = k if k < 9 else 0
+        q = g.sync if k % 2 == 0 else g.scalar
+        q.dma_start(T.win[k::16, 0:1536 - sh], T.strm[:, sh:1536]).then_inc(S.lwin, 16)
+    g.sync.dma_start(T.dicb[:], T.dic[:]).then_inc(S.ldic, 16)
+    WANT, WD, WIN, DIC = ("lwant", 16), ("lwd", 16), ("lwin", 256), ("ldic", 16)
+
+    kw = dict(allow_small_or_imprecise_dtypes=True)
+    i_pi = done("g", g.iota(c1("pi"), [[0, 1]], 0, 1))
+    i_pif = done("g", g.iota(c1("pif"), [[0, 1]], 0, 1, **kw))
+    i_xs = done("g", g.iota(T.xs[:], [[1, 160]], -16, 0, **kw))
+    i_uu = done("g", g.iota(T.uu[:], [[-16, 8], [0, 16]], 0, 1, **kw))
+    i_k8 = done("g", g.iota(T.k8[:], [[0, 4], [1, 8]], 0, 0))
+    i_cb = done("g", g.iota(T.cb[:], [[16, 16]], 0, 0, **kw))
+    col = T.xs[:, 16:144]
+
+    z_e = done("v", V.memset(T.epad[:, 0:24], 0.0))
+    z_c = done("v", V.memset(T.cs[:, 0:1], 0.0))
+    z_t = done("v", V.memset(T.twos[:], 2.0))
+    pm = ts(c1("pm"), c1("pi"), 15, OP.bitwise_and, after=[i_pi])
+    tbl = scan(T.tbl[:], T.twos[:], T.twos[:], 2.0 ** -10, OP.mult, OP.min, after=[z_t])
+    pf = cp(c1("pf"), c1("pm"), after=[pm])
+    idm = ts(T.idm[:], col, c1("pif"), OP.is_equal, 128.0, OP.mult, after=[i_pif, i_xs])
+    lf = ts(T.lf[:], col, c1("pif"), OP.is_gt)
+    rp0 = ts(T.repl[:, 0:1], c1("pf"), 8.0, OP.is_ge, after=[pf])
+    rp1 = ts(T.repl[:, 1:2], c1("pf"), 8.0, OP.is_ge, 2.0, OP.add)
+    d1e = ts(T.d1e[:], T.xs[:], 0.0625, OP.mult, c1("pf"), OP.is_equal)
+    bd = ts(T.bd[:], T.uu[:], c1("pf"), OP.is_equal, after=[i_uu])
+    d0 = act(T.d0[:], T.d1e[:, 0:144], AF.Identity, after=[d1e], bias=0.5, scale=-0.5)
+    maskf = act(T.maskf[:], T.bd[:, 0::16], AF.Copy, after=[bd])
+    g16m = ts(c1("g16m"), c1("pif"), c1("pf"), OP.subtract, -128.0, OP.add)
+    seg = ts(T.seg[:], T.k8[:], 0.0, OP.not_equal, after=[i_k8])
+    ll = tt(T.ll[:], T.lf[:], T.bd[:], OP.mult, after=[lf, bd])
+    xl0 = ts(T.xl[:, 0:8], T.xs[:, 18:26], c1("pf"), OP.mult, 8.0, OP.add)
+    xl1 = ts(T.xl[:, 8:16], T.xs[:, 18:26], c1("pf"), OP.mult)
+    ccol = ts(c1("ccol"), c1("pf"), 15.0, OP.is_equal, -127.0 / 256.0, OP.mult)
+    t2 = scan(T.t2[:], T.d0[:], T.d1e[:, 16:160], 0.0, OP.mult, OP.add, after=[d0])
+
+    wwin = T.wantb[:, 0:4]
+    qrep = ts(T.qrep[:], wwin.indirect(T.repl[:, 0:2]), 7, OP.logical_shift_right, after=[WANT, rp1])
+    brep = ts(T.brep[:], wwin.indirect(T.repl[:, 0:2]), 127, OP.bitwise_and)
+    wb = cp(T.wb[:], T.wdb[:], after=[WD])
+    E = T.epad[:, 24:56]
+    e = tt(E, T.qrep[:], T.k8[:], OP.is_equal, after=[qrep])
+    p1 = group(T.ps1[:, 0:32], [(T.ll[:], E), (T.idm[:], E)] +
+               [(T.bd[:], T.epad[:, 24 - 8 * k:56 - 8 * k]) for k in (1, 2, 3)], after=[e])
+    cs = scan(T.cs[:, 1:8], T.seg[:, 1:8], T.wb[:, 0:7], 0.0, OP.mult, OP.add, after=[wb])
+    wb2 = ts(T.wb2[:], T.wdb[:], 1.0 / 256.0, OP.mult)
+    eb = tt(T.eb[:], E, T.brep[:], OP.mult, after=[e])
+    group(T.ps4[:, 0:8], [(T.ll[:], T.wb[:]), (T.bd[:], T.cs[:])], after=[wb2])
+    p4 = group(T.ps4[:, 8:16], [(T.ll[:], T.wb[:]), (T.idm[:], T.wb2[:]), (T.bd[:], T.cs[:])])
+    ss = scan(T.ss[:], T.seg[:], T.ps1[:, 0:32], 0.0, OP.mult, OP.max, after=[p1])
+    cc0 = ts(T.cc[:, 0:128], T.t2[:].indirect(T.xl[:, 0:8]), 256.0, OP.mult, c1("ccol"), OP.add, after=[t2])
+    for c in range(4):
+        lh = ts(T.lh[:, c, :], col, T.ss[:, 8 * c + 7:8 * c + 8], OP.subtract, c1("g16m"), OP.is_equal, after=[ss])
+    p2 = group(T.ps2[:, 0:8], [(T.lh[:, c, :], T.eb[:, 8 * c:8 * c + 8]) for c in range(4)], after=[lh])
+    cc1 = ts(T.cc[:, 128:256], T.t2[:].indirect(T.xl[:, 8:16]), 256.0, OP.mult)
+    req = cp(T.req[:], T.ps2[:, 0:8], after=[p2])
+
+    plan = {c: calls_of(c, cores, topo) for c in cores}
+    arrive = sum(len(es) for c in cores for call in plan[c] for d, es in call if d == core)
+    sent = [0]
+
+    def exchange(sem, src_of, dst_of):
+        for call in plan[core]:
+            trs = []
+            for d, es in call:
+                rid, pid, _ = topo.addr(d)
+                o = cores.index(d)
+                trs.append(RemoteDMATransfer(dst_ids=[DstId(rid=rid, pnc=pid)], dma_engine_mask=bits(es),
+                                             remote_sem=sem, src=src_of(o), dst=dst_of(o)))
+                sent[0] += len(es)
+            g.remote_dma_fused(trs, local_sem=S.sent)
+
+    need("g", req)
+    exchange(S.rq, lambda o: T.req[:, o:o + 1],
+             lambda o: T.reqin[:, (r - o) % N - 1:(r - o) % N])
+
+    for k in range(8):
+        sm = act(T.sm[:, :, 16 * k:16 * k + 16], T.cc[:], AF.Copy, after=[cc1, maskf], scale=T.maskf[:, k:k + 1])
+
+    stl = ts(T.stl[:], T.ps4[:, 0:16], 2.0, OP.mult, after=[p4])
+    cbs = ts(T.cbs[:], T.cb[:], c1("pf"), OP.add, 1.0 / 128.0, OP.mult, after=[i_cb])
+    onec = ts(c1("onec"), c1("pf"), 15.0, OP.is_equal)
+    maskc = ts(c1("maskc"), c1("pf"), 15.0, OP.not_equal)
+    ownl = cp(T.ownl[:, 0:1], T.ps2[:, r:r + 1])
+    lw = cp(T.lw[:], T.wdb[:])
+    for h in range(2):
+        p5 = group(T.ps5[:, 8 * h:8 * h + 8],
+                   [(T.idm[:], T.wb[:]), (T.idm[:], T.wb[:]), (T.idm[:], T.cbs[:, 8 * h:8 * h + 8])], after=[cbs])
+
+    M = 1.5 * 2.0 ** 31
+    xw = T.win[:].indirect(T.stl[:])
+    hit = ts(T.hit[:], xw, -127.5, OP.add, M, OP.add, after=[WIN, stl])
+    loi = ts(T.loi[:], T.win[:].indirect(T.stl[:]), 255, OP.bitwise_and)
+    hib = act(T.hib[:], T.hit[:], AF.Identity, after=[hit], bias=-M / 256.0, scale=1.0 / 256.0)
+    sel = ts(T.sel[:], T.ps5[:, 0:16], -512.0, OP.add, after=[p5])
+    lob = ts(T.lob[:], T.loi[:], c1("maskc"), OP.mult, c1("onec"), OP.add, after=[loi])
+    evs = []
+    for bank in range(4):
+        ps = T["e%d" % bank]
+        for j in range(2):
+            m = 2 * bank + j
+            pe = group(ps[:, 256 * j:256 * j + 256], [(T.sm[:, 8 + m, :], T.hib[:]), (T.sm[:, m, :], T.lob[:])],
+                       after=[lob, hib, sm])
+        for j in range(2):
+            m = 2 * bank + j
+            sc = 2.0 ** (7 - m)
+            o, i = T.ev[:, 256 * m:256 * m + 256], ps[:, 256 * j:256 * j + 256]
+            if bank % 2 == 0:
+                evs.append(act(o, i, AF.Identity, after=[pe], bias=1.5 * 2.0 ** 23 * sc, scale=sc))
+            else:
+                evs.append(ts(o, i, sc, OP.mult, 1.5 * 2.0 ** 23 * sc, OP.add, after=[pe]))
+    ai = cp(T.ai[:], T.ev[:].indirect(T.sel[:]), after=evs)
+    ui = ts(T.ui[:], T.ai[:], 511, OP.bitwise_and, after=[ai])
+    dd1 = tt(T.dd[:, 128:256], T.tbl[:].indirect(T.lw[:]), T.ui[:, 128:256], OP.mult, after=[ui])
+    dd0 = tt(T.dd[:, 0:128], T.tbl[:].indirect(T.lw[:]), T.ui[:, 0:128], OP.mult)
+
+    RQ, DAT = ("rq", arrive), ("dat", arrive)
+    o1 = act(T.outb[:, 1::2], T.dd[:, 128:256].indirect(T.reqin[:, 0:7]), AF.Identity, after=[dd1, RQ], bias=-256.0)
+    o0 = ts(T.outb[:, 0::2], T.dd[:, 0:128].indirect(T.reqin[:, 0:7]), -256.0, OP.add, after=[dd0, RQ])
+    need("g", o0, o1)
+    exchange(S.dat, lambda o: T.outb[:, 32 * ((o - r) % N - 1):32 * ((o - r) % N - 1) + 24],
+             lambda o: T.land[:, 24 * ((r - o - 1) % N):24 * ((r - o - 1) % N) + 24])
+
+    w0 = ts(T.land[:, 168:200:2], T.dd[:, 0:128].indirect(T.ownl[:, 0:1]), -256.0, OP.add)
+    w1 = ts(T.land[:, 169:200:2], T.dd[:, 128:256].indirect(T.ownl[:, 0:1]), -256.0, OP.add, after=[w0])
+    b1 = ts(T.b1[:], T.k8[:], float(N - 1 - r), OP.add)
+    b2 = ts(T.b2[:], T.b1[:], N - 1, OP.bitwise_and, after=[b1])
+    b3 = ts(T.b3[:], T.b2[:], 12.0, OP.mult, after=[b2])
+    b4 = tt(T.b4[:], T.ps1[:, 0:32], T.b3[:], OP.add, after=[b3])
+    s2 = scan(T.s2[:], T.seg[:], T.b4[:], 0.0, OP.mult, OP.max, after=[b4])
+    ts(T.pos[:, 0:4], T.s2[:, 7::8], 2.0, OP.mult, -256.0, OP.add, after=[s2])
+    pos = ts(T.pos[:, 4:8], T.s2[:, 7::8], 2.0, OP.mult, -255.0, OP.add)
+
+    ts(T.offs[:, 0::2], T.land[:].indirect(T.pos[:, 0:4]), 256.0, OP.add, after=[pos, DAT])
+    of = ts(T.offs[:, 1::2], T.land[:].indirect(T.pos[:, 4:8]), 256.0, OP.add)
+    at = 0
+    nst = 0
+    for n in (16, 24, 24):
+        for q in ("a", "v"):
+            src = T.dicb[:].indirect(T.offs[:, at:at + n])
+            o = T.yb[:, 16 * at:16 * (at + n)]
+            if q == "a":
+                t = act(o, src, AF.Copy, after=[of, DIC])
+            else:
+                t = cp(o, src, after=[of, DIC])
+            need("s", t)
+            g.sync.dma_start(T.y[:, 16 * at:16 * (at + n)], o).then_inc(S.stored, 16)
+            nst += 16
+            at += n
+    need("s", ("stored", nst))
+    need("g", ("sent", sent[0]), ("cg", cnt["g"]), ("cp", cnt["p"]), ("cv", cnt["v"]), ("ca", cnt["a"]))

@@ -11,7 +11,7 @@ SCRATCH = {
     "pif": ("sbuf", [128, 8], "float32"),
     "pm": ("sbuf", [128, 8], "int32"),
     "pf": ("sbuf", [128, 8], "float32"),
-    "g16m": ("sbuf", [128, 8], "float32"),
+    "g16m": ("sbuf", [128, 16], "bfloat16"),
     "onec": ("sbuf", [128, 8], "float32"),
     "maskc": ("sbuf", [128, 8], "float32"),
     "ccol": ("sbuf", [128, 8], "float32"),
@@ -39,7 +39,7 @@ SCRATCH = {
     "brep": ("sbuf", [128, 32], "int32"),
     "epad": ("sbuf", [128, 56], "bfloat16"),
     "eb": ("sbuf", [128, 32], "bfloat16"),
-    "ss": ("sbuf", [128, 32], "float32"),
+    "ss": ("sbuf", [128, 32], "bfloat16"),
     "lh": ("sbuf", [128, 4, 128], "bfloat16"),
     "req": ("sbuf", [128, 8], "uint16"),
     "ownl": ("sbuf", [128, 8], "uint16"),
@@ -48,8 +48,10 @@ SCRATCH = {
     "wb2": ("sbuf", [128, 8], "bfloat16"),
     "cs": ("sbuf", [128, 8], "bfloat16"),
     "lw": ("sbuf", [128, 8], "uint16"),
+    "lw2": ("sbuf", [128, 8], "uint16"),
+    "mup": ("sbuf", [128, 128], "float32"),
     "stl": ("sbuf", [128, 16], "uint16"),
-    "sel": ("sbuf", [128, 16], "uint16"),
+    "sel": ("sbuf", [128, 8], "uint16"),
     "loi": ("sbuf", [128, 256], "int32"),
     "hit": ("sbuf", [128, 256], "float32"),
     "lob": ("sbuf", [128, 256], "bfloat16"),
@@ -60,23 +62,17 @@ SCRATCH = {
     "dd": ("sbuf", [128, 256], "float32"),
     "outb": ("sbuf", [128, 224], "bfloat16"),
     "land": ("sbuf", [128, 200], "bfloat16"),
-    "b1": ("sbuf", [128, 32], "int32"),
-    "b2": ("sbuf", [128, 32], "int32"),
-    "b3": ("sbuf", [128, 32], "float32"),
-    "b4": ("sbuf", [128, 32], "float32"),
-    "s2": ("sbuf", [128, 32], "float32"),
+    "b0": ("sbuf", [128, 4], "int32"),
+    "b1": ("sbuf", [128, 4], "int32"),
+    "b2": ("sbuf", [128, 4], "int32"),
+    "b3": ("sbuf", [128, 4], "float32"),
+    "b4": ("sbuf", [128, 4], "float32"),
     "pos": ("sbuf", [128, 8], "uint16"),
     "offs": ("sbuf", [128, 128], "uint16"),
     "yb": ("sbuf", [128, 2048], "bfloat16"),
-    "ps1": ("psum", [128, 512], "float32"),
-    "ps2": ("psum", [128, 512], "float32"),
-    "ps4": ("psum", [128, 512], "float32"),
-    "ps5": ("psum", [128, 512], "float32"),
-    "e0": ("psum", [128, 512], "float32"),
-    "e1": ("psum", [128, 512], "float32"),
-    "e2": ("psum", [128, 512], "float32"),
-    "e3": ("psum", [128, 512], "float32"),
 }
+for _b in range(8):
+    SCRATCH["e%d" % _b] = ("psum", [128, 512], "float32")
 SEMAPHORES = ["cv", "ca", "cp", "cg", "lwant", "lwd", "lwin", "ldic", "rq", "dat", "sent", "stored"]
 
 
@@ -149,11 +145,13 @@ def rank_program(g, core, T, topo):
 
     def group(out, pairs, after=()):
         need("p", *after)
-        for i, (l, rhs) in enumerate(pairs):
-            ins = P.matmul(out, l, rhs, i == 0, i == len(pairs) - 1)
+        for i, pr in enumerate(pairs):
+            need("p", *pr[2:])
+            ins = P.matmul(out, pr[0], pr[1], i == 0, i == len(pairs) - 1)
         return done("p", ins)
 
     c1 = lambda name: T[name][:, 0:1]
+    ps1, ps2, ps4, ps5 = T.e4, T.e5, T.e6, T.e7
 
     tail = done("v", V.memset(T.win[:, 1528:1536], 0))
     g.sync.dma_start(T.wantb[:, 0:4], T.want[:]).then_inc(S.lwant, 16)
@@ -164,7 +162,6 @@ def rank_program(g, core, T, topo):
         sh = k if k < 9 else 0
         q = g.sync if k % 2 == 0 else g.scalar
         q.dma_start(T.win[k::16, 0:1536 - sh], T.strm[:, sh:1536]).then_inc(S.lwin, 16)
-    g.sync.dma_start(T.dicb[:], T.dic[:]).then_inc(S.ldic, 16)
     WANT, WD, WIN, DIC = ("lwant", 16), ("lwd", 16), ("lwin", 256), ("ldic", 16)
 
     kw = dict(allow_small_or_imprecise_dtypes=True)
@@ -173,51 +170,55 @@ def rank_program(g, core, T, topo):
     i_xs = done("g", g.iota(T.xs[:], [[1, 160]], -16, 0, **kw))
     i_uu = done("g", g.iota(T.uu[:], [[-16, 8], [0, 16]], 0, 1, **kw))
     i_k8 = done("g", g.iota(T.k8[:], [[0, 4], [1, 8]], 0, 0))
-    i_cb = done("g", g.iota(T.cb[:], [[16, 16]], 0, 0, **kw))
+    i_cb = done("g", g.iota(T.cb[:, 0:8], [[16, 8]], 0, 0, **kw))
     col = T.xs[:, 16:144]
 
     z_e = done("v", V.memset(T.epad[:, 0:24], 0.0))
     z_c = done("v", V.memset(T.cs[:, 0:1], 0.0))
-    z_t = done("v", V.memset(T.twos[:], 2.0))
     pm = ts(c1("pm"), c1("pi"), 15, OP.bitwise_and, after=[i_pi])
-    tbl = scan(T.tbl[:], T.twos[:], T.twos[:], 2.0 ** -10, OP.mult, OP.min, after=[z_t])
+    z_t = done("v", V.memset(T.twos[:], 2.0))
     pf = cp(c1("pf"), c1("pm"), after=[pm])
-    idm = ts(T.idm[:], col, c1("pif"), OP.is_equal, 128.0, OP.mult, after=[i_pif, i_xs])
-    lf = ts(T.lf[:], col, c1("pif"), OP.is_gt)
+    tbl = scan(T.tbl[:], T.twos[:], T.twos[:], 2.0 ** -10, OP.mult, OP.min, after=[z_t])
     rp0 = ts(T.repl[:, 0:1], c1("pf"), 8.0, OP.is_ge, after=[pf])
     rp1 = ts(T.repl[:, 1:2], c1("pf"), 8.0, OP.is_ge, 2.0, OP.add)
-    d1e = ts(T.d1e[:], T.xs[:], 0.0625, OP.mult, c1("pf"), OP.is_equal)
+    g16m = ts(c1("g16m"), c1("pif"), c1("pf"), OP.subtract, -128.0, OP.add, after=[i_pif])
+    d1e = ts(T.d1e[:], T.xs[:], 0.0625, OP.mult, c1("pf"), OP.is_equal, after=[i_xs])
+    lf = ts(T.lf[:], col, c1("pif"), OP.is_gt)
+    d0 = ts(T.d0[:], T.d1e[:, 0:144], -0.5, OP.mult, 0.5, OP.add, after=[d1e])
+    idm = ts(T.idm[:], col, c1("pif"), OP.is_equal, 128.0, OP.mult)
     bd = ts(T.bd[:], T.uu[:], c1("pf"), OP.is_equal, after=[i_uu])
-    d0 = act(T.d0[:], T.d1e[:, 0:144], AF.Identity, after=[d1e], bias=0.5, scale=-0.5)
-    maskf = act(T.maskf[:], T.bd[:, 0::16], AF.Copy, after=[bd])
-    g16m = ts(c1("g16m"), c1("pif"), c1("pf"), OP.subtract, -128.0, OP.add)
-    seg = ts(T.seg[:], T.k8[:], 0.0, OP.not_equal, after=[i_k8])
+    t2 = scan(T.t2[:], T.d0[:], T.d1e[:, 16:160], 0.0, OP.mult, OP.add, after=[d0])
     ll = tt(T.ll[:], T.lf[:], T.bd[:], OP.mult, after=[lf, bd])
     xl0 = ts(T.xl[:, 0:8], T.xs[:, 18:26], c1("pf"), OP.mult, 8.0, OP.add)
     xl1 = ts(T.xl[:, 8:16], T.xs[:, 18:26], c1("pf"), OP.mult)
     ccol = ts(c1("ccol"), c1("pf"), 15.0, OP.is_equal, -127.0 / 256.0, OP.mult)
-    t2 = scan(T.t2[:], T.d0[:], T.d1e[:, 16:160], 0.0, OP.mult, OP.add, after=[d0])
+    maskf = act(T.maskf[:], T.bd[:, 0::16], AF.Copy, after=[bd])
+    cc1 = act(T.cc[:, 128:256], T.t2[:].indirect(T.xl[:, 8:16]), AF.Copy, after=[xl1], scale=256.0)
+    cc0 = act(T.cc[:, 0:128], T.t2[:].indirect(T.xl[:, 0:8]), AF.Identity, after=[ccol], bias=c1("ccol"), scale=256.0)
+    for k in range(4):
+        sma = act(T.sm[:, :, 16 * k:16 * k + 16], T.cc[:], AF.Copy, after=[cc0, maskf], scale=T.maskf[:, k:k + 1])
 
     wwin = T.wantb[:, 0:4]
     qrep = ts(T.qrep[:], wwin.indirect(T.repl[:, 0:2]), 7, OP.logical_shift_right, after=[WANT, rp1])
     brep = ts(T.brep[:], wwin.indirect(T.repl[:, 0:2]), 127, OP.bitwise_and)
-    wb = cp(T.wb[:], T.wdb[:], after=[WD])
     E = T.epad[:, 24:56]
-    e = tt(E, T.qrep[:], T.k8[:], OP.is_equal, after=[qrep])
-    p1 = group(T.ps1[:, 0:32], [(T.ll[:], E), (T.idm[:], E)] +
+    e = tt(E, T.qrep[:], T.k8[:], OP.is_equal, after=[qrep, i_k8])
+    p1 = group(ps1[:, 0:32], [(T.ll[:], E), (T.idm[:], E)] +
                [(T.bd[:], T.epad[:, 24 - 8 * k:56 - 8 * k]) for k in (1, 2, 3)], after=[e])
-    cs = scan(T.cs[:, 1:8], T.seg[:, 1:8], T.wb[:, 0:7], 0.0, OP.mult, OP.add, after=[wb])
-    wb2 = ts(T.wb2[:], T.wdb[:], 1.0 / 256.0, OP.mult)
+    seg = ts(T.seg[:], T.k8[:], 0.0, OP.not_equal)
+    wb = cp(T.wb[:], T.wdb[:], after=[WD])
     eb = tt(T.eb[:], E, T.brep[:], OP.mult, after=[e])
-    group(T.ps4[:, 0:8], [(T.ll[:], T.wb[:]), (T.bd[:], T.cs[:])], after=[wb2])
-    p4 = group(T.ps4[:, 8:16], [(T.ll[:], T.wb[:]), (T.idm[:], T.wb2[:]), (T.bd[:], T.cs[:])])
-    ss = scan(T.ss[:], T.seg[:], T.ps1[:, 0:32], 0.0, OP.mult, OP.max, after=[p1])
-    cc0 = ts(T.cc[:, 0:128], T.t2[:].indirect(T.xl[:, 0:8]), 256.0, OP.mult, c1("ccol"), OP.add, after=[t2])
-    for c in range(4):
-        lh = ts(T.lh[:, c, :], col, T.ss[:, 8 * c + 7:8 * c + 8], OP.subtract, c1("g16m"), OP.is_equal, after=[ss])
-    p2 = group(T.ps2[:, 0:8], [(T.lh[:, c, :], T.eb[:, 8 * c:8 * c + 8]) for c in range(4)], after=[lh])
-    cc1 = ts(T.cc[:, 128:256], T.t2[:].indirect(T.xl[:, 8:16]), 256.0, OP.mult)
-    req = cp(T.req[:], T.ps2[:, 0:8], after=[p2])
+    ss = scan(T.ss[:], T.seg[:], ps1[:, 0:32], 0.0, OP.mult, OP.max, after=[p1, seg])
+    cs = scan(T.cs[:, 1:8], T.seg[:, 1:8], T.wb[:, 0:7], 0.0, OP.mult, OP.add, after=[wb])
+    lh = [ts(T.lh[:, c, :], col, T.ss[:, 8 * c + 7:8 * c + 8], OP.subtract, c1("g16m"), OP.is_equal, after=[ss])
+          for c in range(4)]
+    p2 = group(ps2[:, 0:8], [(T.lh[:, c, :], T.eb[:, 8 * c:8 * c + 8], lh[c]) for c in range(4)])
+    wb2 = ts(T.wb2[:], T.wdb[:], 1.0 / 256.0, OP.mult)
+    cbs = ts(T.cbs[:, 0:8], T.cb[:, 0:8], c1("pf"), OP.add, 1.0 / 128.0, OP.mult, after=[i_cb])
+    req = cp(T.req[:], ps2[:, 0:8], after=[p2])
+    group(ps4[:, 0:8], [(T.ll[:], T.wb[:]), (T.bd[:], T.cs[:])], after=[wb2])
+    p4 = group(ps4[:, 8:16], [(T.ll[:], T.wb[:]), (T.idm[:], T.wb2[:]), (T.bd[:], T.cs[:])])
+    p5 = group(ps5[:, 0:8], [(T.idm[:], T.wb[:]), (T.idm[:], T.cbs[:, 0:8])], after=[cbs])
 
     plan = {c: calls_of(c, cores, topo) for c in cores}
     arrive = sum(len(es) for c in cores for call in plan[c] for d, es in call if d == core)
@@ -238,78 +239,93 @@ def rank_program(g, core, T, topo):
     exchange(S.rq, lambda o: T.req[:, o:o + 1],
              lambda o: T.reqin[:, (r - o) % N - 1:(r - o) % N])
 
-    for k in range(8):
-        sm = act(T.sm[:, :, 16 * k:16 * k + 16], T.cc[:], AF.Copy, after=[cc1, maskf], scale=T.maskf[:, k:k + 1])
-
-    stl = ts(T.stl[:], T.ps4[:, 0:16], 2.0, OP.mult, after=[p4])
-    cbs = ts(T.cbs[:], T.cb[:], c1("pf"), OP.add, 1.0 / 128.0, OP.mult, after=[i_cb])
+    lw = cp(T.lw[:], T.wdb[:])
+    lw2 = ts(T.lw2[:], T.wdb[:], -1.0, OP.mult, 11.0, OP.add)
+    stl = ts(T.stl[:], ps4[:, 0:16], 2.0, OP.mult, after=[p4])
+    mup = act(T.mup[:], T.tbl[:].indirect(T.lw2[:]), AF.Copy, after=[lw2], scale=128.0)
+    for k in range(4, 8):
+        smv = ts(T.sm[:, :, 16 * k:16 * k + 16], T.cc[:], T.bd[:, 16 * k:16 * k + 1], OP.mult, after=[cc0])
     onec = ts(c1("onec"), c1("pf"), 15.0, OP.is_equal)
     maskc = ts(c1("maskc"), c1("pf"), 15.0, OP.not_equal)
-    ownl = cp(T.ownl[:, 0:1], T.ps2[:, r:r + 1])
-    lw = cp(T.lw[:], T.wdb[:])
-    for h in range(2):
-        p5 = group(T.ps5[:, 8 * h:8 * h + 8],
-                   [(T.idm[:], T.wb[:]), (T.idm[:], T.wb[:]), (T.idm[:], T.cbs[:, 8 * h:8 * h + 8])], after=[cbs])
+    ownl = cp(T.ownl[:, 0:1], ps2[:, r:r + 1])
+    sel = ts(T.sel[:], ps5[:, 0:8], -256.0, OP.add, after=[p5])
 
     M = 1.5 * 2.0 ** 31
-    xw = T.win[:].indirect(T.stl[:])
-    hit = ts(T.hit[:], xw, -127.5, OP.add, M, OP.add, after=[WIN, stl])
-    loi = ts(T.loi[:], T.win[:].indirect(T.stl[:]), 255, OP.bitwise_and)
-    hib = act(T.hib[:], T.hit[:], AF.Identity, after=[hit], bias=-M / 256.0, scale=1.0 / 256.0)
-    sel = ts(T.sel[:], T.ps5[:, 0:16], -512.0, OP.add, after=[p5])
-    lob = ts(T.lob[:], T.loi[:], c1("maskc"), OP.mult, c1("onec"), OP.add, after=[loi])
-    evs = []
-    for bank in range(4):
-        ps = T["e%d" % bank]
+    MF = 1.5 * 2.0 ** 23
+    hib, lob = [], []
+    for h in range(2):
+        cs_ = slice(128 * h, 128 * h + 128)
+        lst = T.stl[:, 8 * h:8 * h + 8]
+        hit = ts(T.hit[:, cs_], T.win[:].indirect(lst), -127.5, OP.add, M, OP.add, after=[WIN, stl, sel])
+        loi = ts(T.loi[:, cs_], T.win[:].indirect(lst), 255, OP.bitwise_and)
+        hib.append(act(T.hib[:, cs_], T.hit[:, cs_], AF.Identity, after=[hit], bias=-M / 256.0, scale=1.0 / 256.0))
+        lob.append(ts(T.lob[:, cs_], T.loi[:, cs_], c1("maskc"), OP.mult, c1("onec"), OP.add, after=[loi]))
+    need("s", lob[1])
+    g.sync.dma_start(T.dicb[:], T.dic[:]).then_inc(S.ldic, 16)
+
+    pe = []
+    need("p", sma, smv, hib[0])
+    for b in range(4):
+        P.matmul(T["e%d" % b][:, 0:128], T.sm[:, 8 + 2 * b, :], T.hib[:, 0:128], True, False)
+    need("p", lob[0])
+    for b in range(4):
+        ps = T["e%d" % b]
+        P.matmul(ps[:, 0:128], T.sm[:, 2 * b, :], T.lob[:, 0:128], False, True)
+        pe.append(group(ps[:, 128:256], [(T.sm[:, 9 + 2 * b, :], T.hib[:, 0:128]), (T.sm[:, 1 + 2 * b, :], T.lob[:, 0:128])]))
+    for b in range(4):
+        ps = T["e%d" % (4 + b)]
         for j in range(2):
-            m = 2 * bank + j
-            pe = group(ps[:, 256 * j:256 * j + 256], [(T.sm[:, 8 + m, :], T.hib[:]), (T.sm[:, m, :], T.lob[:])],
-                       after=[lob, hib, sm])
-        for j in range(2):
-            m = 2 * bank + j
-            sc = 2.0 ** (7 - m)
-            o, i = T.ev[:, 256 * m:256 * m + 256], ps[:, 256 * j:256 * j + 256]
-            if bank % 2 == 0:
-                evs.append(act(o, i, AF.Identity, after=[pe], bias=1.5 * 2.0 ** 23 * sc, scale=sc))
-            else:
-                evs.append(ts(o, i, sc, OP.mult, 1.5 * 2.0 ** 23 * sc, OP.add, after=[pe]))
-    ai = cp(T.ai[:], T.ev[:].indirect(T.sel[:]), after=evs)
-    ui = ts(T.ui[:], T.ai[:], 511, OP.bitwise_and, after=[ai])
-    dd1 = tt(T.dd[:, 128:256], T.tbl[:].indirect(T.lw[:]), T.ui[:, 128:256], OP.mult, after=[ui])
-    dd0 = tt(T.dd[:, 0:128], T.tbl[:].indirect(T.lw[:]), T.ui[:, 0:128], OP.mult)
+            m = 2 * b + j
+            t = group(ps[:, 128 * j:128 * j + 128],
+                      [(T.sm[:, 8 + m, :], T.hib[:, 128:256]), (T.sm[:, m, :], T.lob[:, 128:256])], after=[hib[1], lob[1]])
+        pe.append(t)
+
+    def evac(b, q):
+        o, i = T.ev[:, 256 * b:256 * b + 256], T["e%d" % b][:, 0:256]
+        if q == "a":
+            return act(o, i, AF.Identity, after=[pe[b]], bias=MF)
+        return ts(o, i, MF, OP.add, after=[pe[b]])
+
+    def post(h, evs):
+        cs_ = slice(128 * h, 128 * h + 128)
+        ai = tt(T.ai[:, cs_], T.ev[:, 1024 * h:1024 * h + 1024].indirect(T.sel[:]), T.mup[:], OP.mult, after=evs)
+        ui = ts(T.ui[:, cs_], T.ai[:, cs_], 511, OP.bitwise_and, after=[ai])
+        return tt(T.dd[:, cs_], T.tbl[:].indirect(T.lw[:]), T.ui[:, cs_], OP.mult, after=[ui])
+
+    dd0 = post(0, [mup, evac(0, "a"), evac(1, "a"), evac(2, "a"), evac(3, "v")])
+    dd1 = post(1, [evac(4, "a"), evac(5, "a"), evac(6, "a"), evac(7, "v")])
 
     RQ, DAT = ("rq", arrive), ("dat", arrive)
-    o1 = act(T.outb[:, 1::2], T.dd[:, 128:256].indirect(T.reqin[:, 0:7]), AF.Identity, after=[dd1, RQ], bias=-256.0)
-    o0 = ts(T.outb[:, 0::2], T.dd[:, 0:128].indirect(T.reqin[:, 0:7]), -256.0, OP.add, after=[dd0, RQ])
+    o0 = act(T.outb[:, 0::2], T.dd[:, 0:128].indirect(T.reqin[:, 0:7]), AF.Identity, after=[dd0, RQ], bias=-256.0)
+    o1 = ts(T.outb[:, 1::2], T.dd[:, 128:256].indirect(T.reqin[:, 0:7]), -256.0, OP.add, after=[dd1, RQ])
     need("g", o0, o1)
     exchange(S.dat, lambda o: T.outb[:, 32 * ((o - r) % N - 1):32 * ((o - r) % N - 1) + 24],
              lambda o: T.land[:, 24 * ((r - o - 1) % N):24 * ((r - o - 1) % N) + 24])
 
     w0 = ts(T.land[:, 168:200:2], T.dd[:, 0:128].indirect(T.ownl[:, 0:1]), -256.0, OP.add)
     w1 = ts(T.land[:, 169:200:2], T.dd[:, 128:256].indirect(T.ownl[:, 0:1]), -256.0, OP.add, after=[w0])
-    b1 = ts(T.b1[:], T.k8[:], float(N - 1 - r), OP.add)
+    b0 = ts(T.b0[:], wwin, 7, OP.logical_shift_right)
+    b1 = ts(T.b1[:], T.b0[:], float(N - 1 - r), OP.add, after=[b0])
     b2 = ts(T.b2[:], T.b1[:], N - 1, OP.bitwise_and, after=[b1])
     b3 = ts(T.b3[:], T.b2[:], 12.0, OP.mult, after=[b2])
-    b4 = tt(T.b4[:], T.ps1[:, 0:32], T.b3[:], OP.add, after=[b3])
-    s2 = scan(T.s2[:], T.seg[:], T.b4[:], 0.0, OP.mult, OP.max, after=[b4])
-    ts(T.pos[:, 0:4], T.s2[:, 7::8], 2.0, OP.mult, -256.0, OP.add, after=[s2])
-    pos = ts(T.pos[:, 4:8], T.s2[:, 7::8], 2.0, OP.mult, -255.0, OP.add)
+    b4 = tt(T.b4[:], T.ss[:, 7::8], T.b3[:], OP.add, after=[b3])
+    ts(T.pos[:, 0:4], T.b4[:], 2.0, OP.mult, -256.0, OP.add, after=[b4])
+    pos = ts(T.pos[:, 4:8], T.b4[:], 2.0, OP.mult, -255.0, OP.add)
 
-    ts(T.offs[:, 0::2], T.land[:].indirect(T.pos[:, 0:4]), 256.0, OP.add, after=[pos, DAT])
-    of = ts(T.offs[:, 1::2], T.land[:].indirect(T.pos[:, 4:8]), 256.0, OP.add)
+    of = []
+    for k in range(2):
+        ts(T.offs[:, 64 * k:64 * k + 64:2], T.land[:].indirect(T.pos[:, 2 * k:2 * k + 2]), 256.0, OP.add, after=[pos, DAT])
+        of.append(ts(T.offs[:, 64 * k + 1:64 * k + 64:2], T.land[:].indirect(T.pos[:, 4 + 2 * k:6 + 2 * k]), 256.0, OP.add))
     at = 0
     nst = 0
-    for n in (16, 24, 24):
-        for q in ("a", "v"):
-            src = T.dicb[:].indirect(T.offs[:, at:at + n])
-            o = T.yb[:, 16 * at:16 * (at + n)]
-            if q == "a":
-                t = act(o, src, AF.Copy, after=[of, DIC])
-            else:
-                t = cp(o, src, after=[of, DIC])
-            need("s", t)
-            g.sync.dma_start(T.y[:, 16 * at:16 * (at + n)], o).then_inc(S.stored, 16)
-            nst += 16
-            at += n
+    for q, n in (("a", 16), ("v", 16), ("a", 26), ("v", 24), ("a", 26), ("v", 20)):
+        src = T.dicb[:].indirect(T.offs[:, at:at + n])
+        o = T.yb[:, 16 * at:16 * (at + n)]
+        dep = [of[0] if at + n <= 64 else of[1], DIC]
+        t = act(o, src, AF.Copy, after=dep) if q == "a" else cp(o, src, after=dep)
+        need("s", t)
+        g.sync.dma_start(T.y[:, 16 * at:16 * (at + n)], o).then_inc(S.stored, 16)
+        nst += 16
+        at += n
     need("s", ("stored", nst))
     need("g", ("sent", sent[0]), ("cg", cnt["g"]), ("cp", cnt["p"]), ("cv", cnt["v"]), ("ca", cnt["a"]))

from concourse.bass import DstId, RemoteDMATransfer
from concourse.mybir import AluOpType as OP, ActivationFunctionType as AF

N = 8
SCRATCH = {
    "win": ("sbuf", [128, 1536], "int32"),
    "wantb": ("sbuf", [128, 8], "int32"),
    "wdb": ("sbuf", [128, 8], "int32"),
    "dicb": ("sbuf", [128, 512], "bfloat16"),
    "pi": ("sbuf", [128, 8], "int32"),
    "pif": ("sbuf", [128, 8], "float32"),
    "pm": ("sbuf", [128, 8], "int32"),
    "pf": ("sbuf", [128, 8], "float32"),
    "g16m": ("sbuf", [128, 16], "bfloat16"),
    "onec": ("sbuf", [128, 8], "float32"),
    "maskc": ("sbuf", [128, 8], "float32"),
    "ccol": ("sbuf", [128, 8], "float32"),
    "repl": ("sbuf", [128, 16], "uint16"),
    "xs": ("sbuf", [128, 160], "bfloat16"),
    "uu": ("sbuf", [128, 128], "bfloat16"),
    "k8": ("sbuf", [128, 32], "int32"),
    "cb": ("sbuf", [128, 16], "float32"),
    "cbs": ("sbuf", [128, 16], "bfloat16"),
    "seg": ("sbuf", [128, 32], "float32"),
    "twos": ("sbuf", [128, 16], "float32"),
    "tbl": ("sbuf", [128, 16], "float32"),
    "bd": ("sbuf", [128, 128], "bfloat16"),
    "lf": ("sbuf", [128, 128], "bfloat16"),
    "ll": ("sbuf", [128, 128], "bfloat16"),
    "idm": ("sbuf", [128, 128], "bfloat16"),
    "maskf": ("sbuf", [128, 8], "float32"),
    "d1e": ("sbuf", [128, 160], "bfloat16"),
    "d0": ("sbuf", [128, 144], "bfloat16"),
    "t2": ("sbuf", [128, 144], "bfloat16"),
    "xl": ("sbuf", [128, 16], "uint16"),
    "cc": ("sbuf", [128, 256], "bfloat16"),
    "sm": ("sbuf", [128, 16, 128], "bfloat16"),
    "qrep": ("sbuf", [128, 32], "int32"),
    "brep": ("sbuf", [128, 32], "int32"),
    "epad": ("sbuf", [128, 56], "bfloat16"),
    "eb": ("sbuf", [128, 32], "bfloat16"),
    "ss": ("sbuf", [128, 32], "bfloat16"),
    "lh": ("sbuf", [128, 4, 128], "bfloat16"),
    "req": ("sbuf", [128, 8], "uint16"),
    "ownl": ("sbuf", [128, 8], "uint16"),
    "reqin": ("sbuf", [128, 8], "uint16"),
    "wb": ("sbuf", [128, 8], "bfloat16"),
    "wb2": ("sbuf", [128, 8], "bfloat16"),
    "cs": ("sbuf", [128, 8], "bfloat16"),
    "lw": ("sbuf", [128, 8], "uint16"),
    "lw2": ("sbuf", [128, 8], "uint16"),
    "mup": ("sbuf", [128, 128], "float32"),
    "stl": ("sbuf", [128, 16], "uint16"),
    "sel": ("sbuf", [128, 8], "uint16"),
    "loi": ("sbuf", [128, 256], "int32"),
    "hit": ("sbuf", [128, 256], "float32"),
    "lob": ("sbuf", [128, 256], "bfloat16"),
    "hib": ("sbuf", [128, 256], "bfloat16"),
    "ev": ("sbuf", [128, 2048], "float32"),
    "ai": ("sbuf", [128, 256], "int32"),
    "ui": ("sbuf", [128, 256], "int32"),
    "dd": ("sbuf", [128, 256], "float32"),
    "outb": ("sbuf", [128, 224], "bfloat16"),
    "land": ("sbuf", [128, 200], "bfloat16"),
    "b0": ("sbuf", [128, 4], "int32"),
    "b1": ("sbuf", [128, 4], "int32"),
    "b2": ("sbuf", [128, 4], "int32"),
    "b3": ("sbuf", [128, 4], "float32"),
    "b4": ("sbuf", [128, 4], "float32"),
    "pos": ("sbuf", [128, 8], "uint16"),
    "offs": ("sbuf", [128, 128], "uint16"),
    "yb": ("sbuf", [128, 2048], "bfloat16"),
}
for _b in range(8):
    SCRATCH["e%d" % _b] = ("psum", [128, 512], "float32")
SEMAPHORES = ["cv", "ca", "cp", "cg", "lwant", "lwd", "lwin", "ldic", "rq", "dat", "sent", "stored"]


def bits(es):
    m = 0
    for e in es:
        m |= 1 << e
    return m


def calls_of(src, cores, topo):
    near = [c for c in cores if c != src and topo.chip(c) == topo.chip(src)]
    far = [c for c in cores if topo.chip(c) != topo.chip(src)]
    far.sort(key=lambda c: topo.same_plane(topo.chip(src), topo.chip(c)))
    e = topo.engines(src, far[0])
    first = [(far[0], e[0:4]), (far[1], e[4:6]), (far[2], e[6:8])]
    second = [(far[4], e[0:2]), (far[5], e[2:4]), (far[3], e[4:8])]
    free = [x for x in topo.engines(src, near[0]) if x not in e]
    second.append((near[0], free[0:2]))
    return [first, second]


def rank_program(g, core, T, topo):
    r = T.rank_of(core)
    if r is None:
        return
    cores = list(T.cores)
    S = T.sem
    Q = {"v": g.vector, "a": g.scalar, "p": g.tensor, "g": g, "s": g.sync}
    cnt = {"v": 0, "a": 0, "p": 0, "g": 0}
    seen = {}

    def need(q, *toks):
        best = {}
        for t in toks:
            best[t[0]] = max(best.get(t[0], 0), t[1])
        for name, n in best.items():
            if seen.get((q, name), 0) < n:
                Q[q].wait_ge(S[name], n)
                seen[(q, name)] = n

    def done(q, ins):
        cnt[q] += 1
        ins.then_inc(S["c" + q], 1)
        return ("c" + q, cnt[q])

    V, A, P = g.vector, g.scalar, g.tensor

    def ts(out, in0, s1, op0, s2=None, op1=None, after=()):
        need("v", *after)
        if op1 is None:
            return done("v", V.tensor_scalar(out, in0, s1, None, op0))
        return done("v", V.tensor_scalar(out, in0, s1, s2, op0, op1))

    def tt(out, in0, in1, op, after=()):
        need("v", *after)
        return done("v", V.tensor_tensor(out, in0, in1, op))

    def cp(out, in_, after=()):
        need("v", *after)
        return done("v", V.tensor_copy(out, in_))

    def scan(out, d0, d1, init, op0, op1, after=()):
        need("v", *after)
        return done("v", V.tensor_tensor_scan(out, d0, d1, init, op0, op1))

    def act(out, in_, func, after=(), **kw):
        need("a", *after)
        return done("a", A.activation(out, in_, func, **kw))

    def group(out, pairs, after=()):
        need("p", *after)
        for i, pr in enumerate(pairs):
            need("p", *pr[2:])
            ins = P.matmul(out, pr[0], pr[1], i == 0, i == len(pairs) - 1)
        return done("p", ins)

    c1 = lambda name: T[name][:, 0:1]
    ps1, ps2, ps4, ps5 = T.e4, T.e5, T.e6, T.e7

    tail = done("v", V.memset(T.win[:, 1528:1536], 0))
    g.sync.dma_start(T.wantb[:, 0:4], T.want[:]).then_inc(S.lwant, 16)
    g.scalar.dma_start(T.wdb[:], T.wd[:]).then_inc(S.lwd, 16)
    need("s", tail)
    need("a", tail)
    for k in range(16):
        sh = k if k < 9 else 0
        q = g.sync if k % 2 == 0 else g.scalar
        q.dma_start(T.win[k::16, 0:1536 - sh], T.strm[:, sh:1536]).then_inc(S.lwin, 16)
    WANT, WD, WIN, DIC = ("lwant", 16), ("lwd", 16), ("lwin", 256), ("ldic", 16)

    kw = dict(allow_small_or_imprecise_dtypes=True)
    i_pi = done("g", g.iota(c1("pi"), [[0, 1]], 0, 1))
    i_pif = done("g", g.iota(c1("pif"), [[0, 1]], 0, 1, **kw))
    i_xs = done("g", g.iota(T.xs[:], [[1, 160]], -16, 0, **kw))
    i_uu = done("g", g.iota(T.uu[:], [[-16, 8], [0, 16]], 0, 1, **kw))
    i_k8 = done("g", g.iota(T.k8[:], [[0, 4], [1, 8]], 0, 0))
    i_cb = done("g", g.iota(T.cb[:, 0:8], [[16, 8]], 0, 0, **kw))
    col = T.xs[:, 16:144]

    z_e = done("v", V.memset(T.epad[:, 0:24], 0.0))
    z_c = done("v", V.memset(T.cs[:, 0:1], 0.0))
    pm = ts(c1("pm"), c1("pi"), 15, OP.bitwise_and, after=[i_pi])
    z_t = done("v", V.memset(T.twos[:], 2.0))
    pf = cp(c1("pf"), c1("pm"), after=[pm])
    tbl = scan(T.tbl[:], T.twos[:], T.twos[:], 2.0 ** -10, OP.mult, OP.min, after=[z_t])
    rp0 = ts(T.repl[:, 0:1], c1("pf"), 8.0, OP.is_ge, after=[pf])
    rp1 = ts(T.repl[:, 1:2], c1("pf"), 8.0, OP.is_ge, 2.0, OP.add)
    g16m = ts(c1("g16m"), c1("pif"), c1("pf"), OP.subtract, -128.0, OP.add, after=[i_pif])
    d1e = ts(T.d1e[:], T.xs[:], 0.0625, OP.mult, c1("pf"), OP.is_equal, after=[i_xs])
    lf = ts(T.lf[:], col, c1("pif"), OP.is_gt)
    d0 = ts(T.d0[:], T.d1e[:, 0:144], -0.5, OP.mult, 0.5, OP.add, after=[d1e])
    idm = ts(T.idm[:], col, c1("pif"), OP.is_equal, 128.0, OP.mult)
    bd = ts(T.bd[:], T.uu[:], c1("pf"), OP.is_equal, after=[i_uu])
    t2 = scan(T.t2[:], T.d0[:], T.d1e[:, 16:160], 0.0, OP.mult, OP.add, after=[d0])
    ll = tt(T.ll[:], T.lf[:], T.bd[:], OP.mult, after=[lf, bd])
    xl0 = ts(T.xl[:, 0:8], T.xs[:, 18:26], c1("pf"), OP.mult, 8.0, OP.add)
    xl1 = ts(T.xl[:, 8:16], T.xs[:, 18:26], c1("pf"), OP.mult)
    ccol = ts(c1("ccol"), c1("pf"), 15.0, OP.is_equal, -127.0 / 256.0, OP.mult)
    maskf = act(T.maskf[:], T.bd[:, 0::16], AF.Copy, after=[bd])
    cc1 = act(T.cc[:, 128:256], T.t2[:].indirect(T.xl[:, 8:16]), AF.Copy, after=[xl1], scale=256.0)
    cc0 = act(T.cc[:, 0:128], T.t2[:].indirect(T.xl[:, 0:8]), AF.Identity, after=[ccol], bias=c1("ccol"), scale=256.0)
    for k in range(4):
        sma = act(T.sm[:, :, 16 * k:16 * k + 16], T.cc[:], AF.Copy, after=[cc0, maskf], scale=T.maskf[:, k:k + 1])

    wwin = T.wantb[:, 0:4]
    qrep = ts(T.qrep[:], wwin.indirect(T.repl[:, 0:2]), 7, OP.logical_shift_right, after=[WANT, rp1])
    brep = ts(T.brep[:], wwin.indirect(T.repl[:, 0:2]), 127, OP.bitwise_and)
    E = T.epad[:, 24:56]
    e = tt(E, T.qrep[:], T.k8[:], OP.is_equal, after=[qrep, i_k8])
    p1 = group(ps1[:, 0:32], [(T.ll[:], E), (T.idm[:], E)] +
               [(T.bd[:], T.epad[:, 24 - 8 * k:56 - 8 * k]) for k in (1, 2, 3)], after=[e])
    seg = ts(T.seg[:], T.k8[:], 0.0, OP.not_equal)
    wb = cp(T.wb[:], T.wdb[:], after=[WD])
    eb = tt(T.eb[:], E, T.brep[:], OP.mult, after=[e])
    ss = scan(T.ss[:], T.seg[:], ps1[:, 0:32], 0.0, OP.mult, OP.max, after=[p1, seg])
    cs = scan(T.cs[:, 1:8], T.seg[:, 1:8], T.wb[:, 0:7], 0.0, OP.mult, OP.add, after=[wb])
    lh = [ts(T.lh[:, c, :], col, T.ss[:, 8 * c + 7:8 * c + 8], OP.subtract, c1("g16m"), OP.is_equal, after=[ss])
          for c in range(4)]
    p2 = group(ps2[:, 0:8], [(T.lh[:, c, :], T.eb[:, 8 * c:8 * c + 8], lh[c]) for c in range(4)])
    wb2 = ts(T.wb2[:], T.wdb[:], 1.0 / 256.0, OP.mult)
    cbs = ts(T.cbs[:, 0:8], T.cb[:, 0:8], c1("pf"), OP.add, 1.0 / 128.0, OP.mult, after=[i_cb])
    req = cp(T.req[:], ps2[:, 0:8], after=[p2])
    group(ps4[:, 0:8], [(T.ll[:], T.wb[:]), (T.bd[:], T.cs[:])], after=[wb2])
    p4 = group(ps4[:, 8:16], [(T.ll[:], T.wb[:]), (T.idm[:], T.wb2[:]), (T.bd[:], T.cs[:])])
    p5 = group(ps5[:, 0:8], [(T.idm[:], T.wb[:]), (T.idm[:], T.cbs[:, 0:8])], after=[cbs])

    plan = {c: calls_of(c, cores, topo) for c in cores}
    arrive = sum(len(es) for c in cores for call in plan[c] for d, es in call if d == core)
    sent = [0]

    def exchange(sem, src_of, dst_of):
        for call in plan[core]:
            trs = []
            for d, es in call:
                rid, pid, _ = topo.addr(d)
                o = cores.index(d)
                trs.append(RemoteDMATransfer(dst_ids=[DstId(rid=rid, pnc=pid)], dma_engine_mask=bits(es),
                                             remote_sem=sem, src=src_of(o), dst=dst_of(o)))
                sent[0] += len(es)
            g.remote_dma_fused(trs, local_sem=S.sent)

    need("g", req)
    exchange(S.rq, lambda o: T.req[:, o:o + 1],
             lambda o: T.reqin[:, (r - o) % N - 1:(r - o) % N])

    lw = cp(T.lw[:], T.wdb[:])
    lw2 = ts(T.lw2[:], T.wdb[:], -1.0, OP.mult, 11.0, OP.add)
    stl = ts(T.stl[:], ps4[:, 0:16], 2.0, OP.mult, after=[p4])
    mup = act(T.mup[:], T.tbl[:].indirect(T.lw2[:]), AF.Copy, after=[lw2], scale=128.0)
    for k in range(4, 8):
        smv = ts(T.sm[:, :, 16 * k:16 * k + 16], T.cc[:], T.bd[:, 16 * k:16 * k + 1], OP.mult, after=[cc0])
    onec = ts(c1("onec"), c1("pf"), 15.0, OP.is_equal)
    maskc = ts(c1("maskc"), c1("pf"), 15.0, OP.not_equal)
    ownl = cp(T.ownl[:, 0:1], ps2[:, r:r + 1])
    sel = ts(T.sel[:], ps5[:, 0:8], -256.0, OP.add, after=[p5])

    M = 1.5 * 2.0 ** 31
    MF = 1.5 * 2.0 ** 23
    hib, lob = [], []
    for h in range(2):
        cs_ = slice(128 * h, 128 * h + 128)
        lst = T.stl[:, 8 * h:8 * h + 8]
        hit = ts(T.hit[:, cs_], T.win[:].indirect(lst), -127.5, OP.add, M, OP.add, after=[WIN, stl, sel])
        loi = ts(T.loi[:, cs_], T.win[:].indirect(lst), 255, OP.bitwise_and)
        hib.append(act(T.hib[:, cs_], T.hit[:, cs_], AF.Identity, after=[hit], bias=-M / 256.0, scale=1.0 / 256.0))
        lob.append(ts(T.lob[:, cs_], T.loi[:, cs_], c1("maskc"), OP.mult, c1("onec"), OP.add, after=[loi]))
    need("s", lob[1])
    g.sync.dma_start(T.dicb[:], T.dic[:]).then_inc(S.ldic, 16)

    pe = []
    need("p", sma, smv, hib[0])
    for b in range(4):
        P.matmul(T["e%d" % b][:, 0:128], T.sm[:, 8 + 2 * b, :], T.hib[:, 0:128], True, False)
    need("p", lob[0])
    for b in range(4):
        ps = T["e%d" % b]
        P.matmul(ps[:, 0:128], T.sm[:, 2 * b, :], T.lob[:, 0:128], False, True)
        pe.append(group(ps[:, 128:256], [(T.sm[:, 9 + 2 * b, :], T.hib[:, 0:128]), (T.sm[:, 1 + 2 * b, :], T.lob[:, 0:128])]))
    for b in range(4):
        ps = T["e%d" % (4 + b)]
        for j in range(2):
            m = 2 * b + j
            t = group(ps[:, 128 * j:128 * j + 128],
                      [(T.sm[:, 8 + m, :], T.hib[:, 128:256]), (T.sm[:, m, :], T.lob[:, 128:256])], after=[hib[1], lob[1]])
        pe.append(t)

    def evac(b, q):
        o, i = T.ev[:, 256 * b:256 * b + 256], T["e%d" % b][:, 0:256]
        if q == "a":
            return act(o, i, AF.Identity, after=[pe[b]], bias=MF)
        return ts(o, i, MF, OP.add, after=[pe[b]])

    def post(h, evs):
        cs_ = slice(128 * h, 128 * h + 128)
        ai = tt(T.ai[:, cs_], T.ev[:, 1024 * h:1024 * h + 1024].indirect(T.sel[:]), T.mup[:], OP.mult, after=evs)
        ui = ts(T.ui[:, cs_], T.ai[:, cs_], 511, OP.bitwise_and, after=[ai])
        return tt(T.dd[:, cs_], T.tbl[:].indirect(T.lw[:]), T.ui[:, cs_], OP.mult, after=[ui])

    dd0 = post(0, [mup, evac(0, "a"), evac(1, "a"), evac(2, "a"), evac(3, "v")])
    dd1 = post(1, [evac(4, "a"), evac(5, "a"), evac(6, "a"), evac(7, "v")])

    RQ, DAT = ("rq", arrive), ("dat", arrive)
    o0 = act(T.outb[:, 0::2], T.dd[:, 0:128].indirect(T.reqin[:, 0:7]), AF.Identity, after=[dd0, RQ], bias=-256.0)
    o1 = ts(T.outb[:, 1::2], T.dd[:, 128:256].indirect(T.reqin[:, 0:7]), -256.0, OP.add, after=[dd1, RQ])
    need("g", o0, o1)
    exchange(S.dat, lambda o: T.outb[:, 32 * ((o - r) % N - 1):32 * ((o - r) % N - 1) + 24],
             lambda o: T.land[:, 24 * ((r - o - 1) % N):24 * ((r - o - 1) % N) + 24])

    w0 = ts(T.land[:, 168:200:2], T.dd[:, 0:128].indirect(T.ownl[:, 0:1]), -256.0, OP.add)
    w1 = ts(T.land[:, 169:200:2], T.dd[:, 128:256].indirect(T.ownl[:, 0:1]), -256.0, OP.add, after=[w0])
    b0 = ts(T.b0[:], wwin, 7, OP.logical_shift_right)
    b1 = ts(T.b1[:], T.b0[:], float(N - 1 - r), OP.add, after=[b0])
    b2 = ts(T.b2[:], T.b1[:], N - 1, OP.bitwise_and, after=[b1])
    b3 = ts(T.b3[:], T.b2[:], 12.0, OP.mult, after=[b2])
    b4 = tt(T.b4[:], T.ss[:, 7::8], T.b3[:], OP.add, after=[b3])
    ts(T.pos[:, 0:4], T.b4[:], 2.0, OP.mult, -256.0, OP.add, after=[b4])
    pos = ts(T.pos[:, 4:8], T.b4[:], 2.0, OP.mult, -255.0, OP.add)

    of = []
    for k in range(2):
        ts(T.offs[:, 64 * k:64 * k + 64:2], T.land[:].indirect(T.pos[:, 2 * k:2 * k + 2]), 256.0, OP.add, after=[pos, DAT])
        of.append(ts(T.offs[:, 64 * k + 1:64 * k + 64:2], T.land[:].indirect(T.pos[:, 4 + 2 * k:6 + 2 * k]), 256.0, OP.add))
    at = 0
    nst = 0
    for q, n in (("a", 16), ("v", 16), ("a", 26), ("v", 24), ("a", 26), ("v", 20)):
        src = T.dicb[:].indirect(T.offs[:, at:at + n])
        o = T.yb[:, 16 * at:16 * (at + n)]
        dep = [of[0] if at + n <= 64 else of[1], DIC]
        t = act(o, src, AF.Copy, after=dep) if q == "a" else cp(o, src, after=dep)
        need("s", t)
        g.sync.dma_start(T.y[:, 16 * at:16 * (at + n)], o).then_inc(S.stored, 16)
        nst += 16
        at += n
    need("s", ("stored", nst))
    need("g", ("sent", sent[0]), ("cg", cnt["g"]), ("cp", cnt["p"]), ("cv", cnt["v"]), ("ca", cnt["a"]))
